import numpy as np
import ml_dtypes


def mxq(x, axis, fmt="e4m3"):
    dtype, down = {"e4m3": (ml_dtypes.float8_e4m3fn, 7), "e5m2": (ml_dtypes.float8_e5m2, 14)}[fmt]
    v = np.moveaxis(np.asarray(x, np.float32).astype(ml_dtypes.bfloat16).astype(np.float64), axis, -1)
    blocks = v.reshape(v.shape[:-1] + (-1, 32))
    amax = np.abs(blocks).max(-1, keepdims=True)
    byte = np.maximum(np.where(amax > 0, np.frexp(amax)[1] - 1 + 127, 0) - down, 1)
    scale = np.exp2(byte - 127.0)
    codes = (blocks / scale).astype(np.float32).astype(dtype).astype(np.float64)
    return np.moveaxis((codes * scale).reshape(v.shape), -1, axis)


WIDE = False


def mx_kscale(k):
    if not WIDE:
        return np.ones(k)
    levels = np.array([10, -10, 5, -5, 0])
    if k % 512:
        return np.exp2(np.random.permutation(np.resize(levels, k // 32))).repeat(32)
    a = np.empty((k // 512, 16))
    for p in range(k // 512):
        a[p, :8] = np.random.permutation(np.resize(levels, 8))
        for g in range(8):
            far = levels[np.abs(levels - a[p, g]) >= 10]
            a[p, g + 8] = far[np.random.randint(len(far))]
    return np.exp2(a.ravel()).repeat(32)


def f64(x):
    return np.asarray(x).astype(np.float64)


def striped(idx):
    return np.tile(np.asarray(idx).reshape(-1, 16).T, (8, 1)).astype(np.uint16)


def unstriped(offs):
    return offs[:16].T.reshape(-1).astype(np.int64)


B, N, C, D, NQ = 1, 256, 4096, 512, 256


def eight(codes):
    return np.concatenate([codes[h].reshape(-1, 16).T for h in range(8)]).astype(np.uint16)


def uneight(offs):
    return np.stack([offs[16 * h:16 * h + 16].T.reshape(-1) for h in range(8)]).astype(np.int64)


def setup_inputs():
    n = np.random.standard_normal
    s = mx_kscale(D)[:, None]
    grid = lambda x: np.round(x * 32) / 32
    return {
        "qT": (n((B, D, NQ)) * s / np.sqrt(D)).astype(np.float32),
        "cb": (grid(n((D, C))) / s).astype(np.float32),
        "norm": np.tile(np.random.randint(32, 129, N) / 64.0, (128, 1)).astype(np.float32),
        "bias": np.tile(n(N), (128, 1)).astype(np.float32),
        "offs": eight(np.random.randint(0, C, (8, N))),
    }


def reference(qT, cb, norm, bias, offs):
    k = []
    for part, offs_ in enumerate((offs,)):
        codes = uneight(offs_)
        k += [f64(cb)[512 * part + 64 * h:512 * part + 64 * h + 64][:, codes[h]] for h in range(8)]
    k = np.concatenate(k) * f64(norm)[:1]
    a = mxq(f64(qT), 1, "e4m3").transpose(0, 2, 1) @ mxq(k, 0, "e4m3")
    a = a + f64(bias)[:1]
    return a

@@ -1,0 +1,107 @@
+import concourse.mybir as mybir
+from concourse.masks import make_identity
+
+F32 = mybir.dt.float32
+BF16 = mybir.dt.bfloat16
+U32 = mybir.dt.uint32
+U16 = mybir.dt.uint16
+U8 = mybir.dt.uint8
+FP8X4 = mybir.dt.float8_e4m3fn_x4
+MULT = mybir.AluOpType.mult
+ADD = mybir.AluOpType.add
+
+P = 128
+PACK = 4
+N = 256
+NQ = 256
+D = 512
+HALF = 128
+FLOPS = 2 * NQ * N * D
+
+
+def tile_attend_pq_lin_bias_kernel(tc, qT, cb, norm, bias, offs, out):
+    nc = tc.nc
+    with (
+        tc.tile_pool(name="keep", bufs=1) as keep,
+        tc.psum_pool(name="psum", bufs=1) as psum,
+    ):
+        planes = [keep.tile([P, 4096], F32, name=f"plane{t}") for t in range(PACK)]
+        lists = keep.tile([P, N // 16], U16, name="lists")
+        norm_sb = keep.tile([P, N], F32, name="norm_sb")
+        bias_sb = keep.tile([P, N], F32, name="bias_sb")
+        q_raw = keep.tile([P, PACK, NQ], F32, name="q_raw")
+
+        norm_rows = keep.tile([P, P], F32, name="norm_rows")
+        identity = keep.tile([P, P], F32, name="identity")
+        nc.gpsimd.memset(norm_rows[:], 0.0)
+        make_identity(nc, identity[:])
+
+        cb_rows = cb.rearrange("(p t) c -> p t c", t=PACK)
+        nc.sync.dma_start(planes[0][:], cb_rows[:, 0, :])
+        nc.sync.dma_start(lists[:], offs)
+        nc.sync.dma_start(norm_rows[0:2, :], norm[0:1, :].rearrange("o (u n) -> (o u) n", u=2))
+        nc.sync.dma_start(q_raw[:], qT[0, :, :].rearrange("(p t) q -> p t q", t=PACK))
+        for t in range(1, PACK):
+            nc.sync.dma_start(planes[t][:], cb_rows[:, t, :])
+        nc.sync.dma_start(bias_sb[:], bias)
+
+        norm_turned = psum.tile([P, P], F32, name="norm_turned")
+        norm_cols = keep.tile([P, 2], F32, name="norm_cols")
+        norm_spread = psum.tile([P, 2, P], F32, name="norm_spread")
+        nc.tensor.transpose(norm_turned[:], norm_rows[:], identity[:])
+        nc.scalar.copy(norm_cols[:], norm_turned[:, 0:2])
+        for u in range(2):
+            nc.tensor.transpose(norm_spread[:, u, :], norm_cols[:, u : u + 1].to_broadcast([P, P]), identity[:])
+        nc.scalar.copy(norm_sb[:], norm_spread[:].rearrange("p u n -> p (u n)"))
+
+        q_grouped = keep.tile([P, NQ, PACK], BF16, name="q_grouped", align_bytes=64)
+        q_codes = keep.tile([P, NQ], U32, name="q_codes", align_bytes=64)
+        q_scales = keep.tile([P, NQ], U8, name="q_scales", align_bytes=64)
+        nc.scalar.copy(q_grouped[:], q_raw[:].rearrange("p t q -> p q t"))
+        nc.vector.quantize_mx(
+            out=q_codes[:].bitcast(FP8X4),
+            scales=q_scales[:],
+            in_=q_grouped[:].rearrange("p q t -> p (q t)"),
+        )
+
+        gathered = [keep.tile([P, PACK, HALF], F32, name=f"gathered{h}") for h in range(2)]
+        grouped = [keep.tile([P, HALF, PACK], BF16, name=f"grouped{h}", align_bytes=64) for h in range(2)]
+        codes = [keep.tile([P, HALF], U32, name=f"codes{h}", align_bytes=64) for h in range(2)]
+        scales = [keep.tile([P, HALF], U8, name=f"scales{h}", align_bytes=64) for h in range(2)]
+        acc = [[psum.tile([P, HALF], F32, name=f"acc{h}{b}") for b in range(2)] for h in range(2)]
+        result = [[keep.tile([P, HALF], F32, name=f"result{h}{b}") for b in range(2)] for h in range(2)]
+
+        for t in range(PACK):
+            for h in range(2):
+                nc.vector.tensor_tensor(
+                    gathered[h][:, t, :],
+                    planes[t][:].indirect(lists[:, 8 * h : 8 * h + 8]),
+                    norm_sb[:, HALF * h : HALF * h + HALF],
+                    MULT,
+                )
+            for h in range(2):
+                nc.vector.tensor_copy(grouped[h][:, :, t], gathered[h][:, t, :])
+        for h in range(2):
+            nc.vector.quantize_mx(
+                out=codes[h][:].bitcast(FP8X4),
+                scales=scales[h][:],
+                in_=grouped[h][:].rearrange("p n t -> p (n t)"),
+            )
+        for h in range(2):
+            for b in range(2):
+                q_cols = slice(P * b, P * b + P)
+                nc.tensor.matmul_mx(
+                    out=acc[h][b][:],
+                    lhsT=q_codes[:, q_cols].bitcast(FP8X4),
+                    lhsT_scale=q_scales[:, q_cols],
+                    rhs=codes[h][:].bitcast(FP8X4),
+                    rhs_scale=scales[h][:],
+                    start=True,
+                    stop=True,
+                )
+        for h in range(2):
+            n_cols = slice(HALF * h, HALF * h + HALF)
+            for b in range(2):
+                nc.vector.tensor_tensor(result[h][b][:], acc[h][b][:], bias_sb[:, n_cols], ADD)
+                store = nc.sync if b == 0 else nc.scalar
+                store.dma_start(out[0, P * b : P * b + P, n_cols], result[h][b][:])

@@ -29,7 +29,7 @@ def tile_attend_pq_lin_bias_kernel(tc, qT, cb, norm, bias, offs, out):
         lists = keep.tile([P, N // 16], U16, name="lists")
         norm_sb = keep.tile([P, N], F32, name="norm_sb")
         bias_sb = keep.tile([P, N], F32, name="bias_sb")
-        q_raw = keep.tile([P, PACK, NQ], F32, name="q_raw")
+        q_raw = [keep.tile([P, PACK, P], F32, name=f"q_raw{b}") for b in range(2)]
 
         norm_rows = keep.tile([P, P], F32, name="norm_rows")
         identity = keep.tile([P, P], F32, name="identity")
@@ -40,9 +40,11 @@ def tile_attend_pq_lin_bias_kernel(tc, qT, cb, norm, bias, offs, out):
         nc.sync.dma_start(planes[0][:], cb_rows[:, 0, :])
         nc.sync.dma_start(lists[:], offs)
         nc.sync.dma_start(norm_rows[0:2, :], norm[0:1, :].rearrange("o (u n) -> (o u) n", u=2))
-        nc.sync.dma_start(q_raw[:], qT[0, :, :].rearrange("(p t) q -> p t q", t=PACK))
         for t in range(1, PACK):
             nc.sync.dma_start(planes[t][:], cb_rows[:, t, :])
+        q_rows = qT[0, :, :].rearrange("(p t) q -> p t q", t=PACK)
+        for b in range(2):
+            nc.sync.dma_start(q_raw[b][:], q_rows[:, :, P * b : P * b + P])
         nc.sync.dma_start(bias_sb[:], bias)
 
         norm_turned = psum.tile([P, P], F32, name="norm_turned")
@@ -54,15 +56,9 @@ def tile_attend_pq_lin_bias_kernel(tc, qT, cb, norm, bias, offs, out):
             nc.tensor.transpose(norm_spread[:, u, :], norm_cols[:, u : u + 1].to_broadcast([P, P]), identity[:])
         nc.scalar.copy(norm_sb[:], norm_spread[:].rearrange("p u n -> p (u n)"))
 
-        q_grouped = keep.tile([P, NQ, PACK], BF16, name="q_grouped", align_bytes=64)
-        q_codes = keep.tile([P, NQ], U32, name="q_codes", align_bytes=64)
-        q_scales = keep.tile([P, NQ], U8, name="q_scales", align_bytes=64)
-        nc.scalar.copy(q_grouped[:], q_raw[:].rearrange("p t q -> p q t"))
-        nc.vector.quantize_mx(
-            out=q_codes[:].bitcast(FP8X4),
-            scales=q_scales[:],
-            in_=q_grouped[:].rearrange("p q t -> p (q t)"),
-        )
+        q_grouped = [keep.tile([P, P, PACK], BF16, name=f"q_grouped{b}", align_bytes=64) for b in range(2)]
+        q_codes = [keep.tile([P, P], U32, name=f"q_codes{b}", align_bytes=64) for b in range(2)]
+        q_scales = [keep.tile([P, P], U8, name=f"q_scales{b}", align_bytes=64) for b in range(2)]
 
         gathered = [keep.tile([P, PACK, HALF], F32, name=f"gathered{h}") for h in range(2)]
         grouped = [keep.tile([P, HALF, PACK], BF16, name=f"grouped{h}", align_bytes=64) for h in range(2)]
@@ -87,21 +83,29 @@ def tile_attend_pq_lin_bias_kernel(tc, qT, cb, norm, bias, offs, out):
                 scales=scales[h][:],
                 in_=grouped[h][:].rearrange("p n t -> p (n t)"),
             )
-        for h in range(2):
-            for b in range(2):
-                q_cols = slice(P * b, P * b + P)
+        nc.scalar.copy(q_grouped[0][:], q_raw[0][:].rearrange("p t q -> p q t"))
+        nc.scalar.copy(q_grouped[1][:, 0:64, :], q_raw[1][:, :, 0:64].rearrange("p t q -> p q t"))
+        nc.vector.tensor_copy(q_grouped[1][:, 64:128, :], q_raw[1][:, :, 64:128].rearrange("p t q -> p q t"))
+        for b in range(2):
+            nc.vector.quantize_mx(
+                out=q_codes[b][:].bitcast(FP8X4),
+                scales=q_scales[b][:],
+                in_=q_grouped[b][:].rearrange("p q t -> p (q t)"),
+            )
+        for b in range(2):
+            for h in range(2):
                 nc.tensor.matmul_mx(
                     out=acc[h][b][:],
-                    lhsT=q_codes[:, q_cols].bitcast(FP8X4),
-                    lhsT_scale=q_scales[:, q_cols],
+                    lhsT=q_codes[b][:].bitcast(FP8X4),
+                    lhsT_scale=q_scales[b][:],
                     rhs=codes[h][:].bitcast(FP8X4),
                     rhs_scale=scales[h][:],
                     start=True,
                     stop=True,
                 )
-        for h in range(2):
-            n_cols = slice(HALF * h, HALF * h + HALF)
-            for b in range(2):
+        for b in range(2):
+            for h in range(2):
+                n_cols = slice(HALF * h, HALF * h + HALF)
                 nc.vector.tensor_tensor(result[h][b][:], acc[h][b][:], bias_sb[:, n_cols], ADD)
-                store = nc.sync if b == 0 else nc.scalar
+                store = nc.scalar if h == 0 else nc.sync
                 store.dma_start(out[0, P * b : P * b + P, n_cols], result[h][b][:])

@@ -16,6 +16,7 @@ N = 256
 NQ = 256
 D = 512
 HALF = 128
+SCALAR_SHARE = 64
 FLOPS = 2 * NQ * N * D
 
 
@@ -56,50 +57,52 @@ def tile_attend_pq_lin_bias_kernel(tc, qT, cb, norm, bias, offs, out):
             nc.tensor.transpose(norm_spread[:, u, :], norm_cols[:, u : u + 1].to_broadcast([P, P]), identity[:])
         nc.scalar.copy(norm_sb[:], norm_spread[:].rearrange("p u n -> p (u n)"))
 
-        q_grouped = [keep.tile([P, P, PACK], BF16, name=f"q_grouped{b}", align_bytes=64) for b in range(2)]
-        q_codes = [keep.tile([P, P], U32, name=f"q_codes{b}", align_bytes=64) for b in range(2)]
-        q_scales = [keep.tile([P, P], U8, name=f"q_scales{b}", align_bytes=64) for b in range(2)]
-
-        gathered = [keep.tile([P, PACK, HALF], F32, name=f"gathered{h}") for h in range(2)]
-        grouped = [keep.tile([P, HALF, PACK], BF16, name=f"grouped{h}", align_bytes=64) for h in range(2)]
-        codes = [keep.tile([P, HALF], U32, name=f"codes{h}", align_bytes=64) for h in range(2)]
-        scales = [keep.tile([P, HALF], U8, name=f"scales{h}", align_bytes=64) for h in range(2)]
+        grouped = keep.tile([P, 4 * P, PACK], BF16, name="grouped", align_bytes=64)
+        codes = keep.tile([P, 4 * P], U32, name="codes", align_bytes=64)
+        scales = keep.tile([P, 4 * P], U8, name="scales", align_bytes=64)
+        gathered = [keep.tile([P, HALF], F32, name=f"gathered{h}") for h in range(2)]
         acc = [[psum.tile([P, HALF], F32, name=f"acc{h}{b}") for b in range(2)] for h in range(2)]
         result = [[keep.tile([P, HALF], F32, name=f"result{h}{b}") for b in range(2)] for h in range(2)]
+
+        def quantize(first, last):
+            nc.vector.quantize_mx(
+                out=codes[:, first:last].bitcast(FP8X4),
+                scales=scales[:, first:last],
+                in_=grouped[:, first:last, :].rearrange("p n t -> p (n t)"),
+            )
+
+        def interleave(copy, b, first, last):
+            copy(
+                grouped[:, N + P * b + first : N + P * b + last, :].rearrange("p (c i) t -> p c t i", i=4),
+                q_raw[b][:, :, first:last].rearrange("p t (c i) -> p c t i", i=4),
+            )
 
         for t in range(PACK):
             for h in range(2):
                 nc.vector.tensor_tensor(
-                    gathered[h][:, t, :],
+                    gathered[h][:],
                     planes[t][:].indirect(lists[:, 8 * h : 8 * h + 8]),
                     norm_sb[:, HALF * h : HALF * h + HALF],
                     MULT,
                 )
             for h in range(2):
-                nc.vector.tensor_copy(grouped[h][:, :, t], gathered[h][:, t, :])
-        for h in range(2):
-            nc.vector.quantize_mx(
-                out=codes[h][:].bitcast(FP8X4),
-                scales=scales[h][:],
-                in_=grouped[h][:].rearrange("p n t -> p (n t)"),
-            )
-        nc.scalar.copy(q_grouped[0][:], q_raw[0][:].rearrange("p t q -> p q t"))
-        nc.scalar.copy(q_grouped[1][:, 0:64, :], q_raw[1][:, :, 0:64].rearrange("p t q -> p q t"))
-        nc.vector.tensor_copy(q_grouped[1][:, 64:128, :], q_raw[1][:, :, 64:128].rearrange("p t q -> p q t"))
+                nc.vector.tensor_copy(grouped[:, HALF * h : HALF * h + HALF, t], gathered[h][:])
+        interleave(nc.scalar.copy, 0, 0, P)
+        interleave(nc.scalar.copy, 1, 0, SCALAR_SHARE)
+        quantize(0, P)
+        interleave(nc.vector.tensor_copy, 1, SCALAR_SHARE, P)
+        quantize(P, 3 * P)
+        quantize(3 * P, 4 * P)
         for b in range(2):
-            nc.vector.quantize_mx(
-                out=q_codes[b][:].bitcast(FP8X4),
-                scales=q_scales[b][:],
-                in_=q_grouped[b][:].rearrange("p q t -> p (q t)"),
-            )
-        for b in range(2):
+            q_cols = slice(N + P * b, N + P * b + P)
             for h in range(2):
+                n_cols = slice(HALF * h, HALF * h + HALF)
                 nc.tensor.matmul_mx(
                     out=acc[h][b][:],
-                    lhsT=q_codes[b][:].bitcast(FP8X4),
-                    lhsT_scale=q_scales[b][:],
-                    rhs=codes[h][:].bitcast(FP8X4),
-                    rhs_scale=scales[h][:],
+                    lhsT=codes[:, q_cols].bitcast(FP8X4),
+                    lhsT_scale=scales[:, q_cols],
+                    rhs=codes[:, n_cols].bitcast(FP8X4),
+                    rhs_scale=scales[:, n_cols],
                     start=True,
                     stop=True,
                 )

@@ -30,7 +30,7 @@ def tile_attend_pq_lin_bias_kernel(tc, qT, cb, norm, bias, offs, out):
         lists = keep.tile([P, N // 16], U16, name="lists")
         norm_sb = keep.tile([P, N], F32, name="norm_sb")
         bias_sb = keep.tile([P, N], F32, name="bias_sb")
-        q_raw = [keep.tile([P, PACK, P], F32, name=f"q_raw{b}") for b in range(2)]
+        q_raw = [keep.tile([P, PACK, P], F32, name=f"q_raw{b}", tag=f"q_raw{b}", align_bytes=64) for b in range(2)]
 
         norm_rows = keep.tile([P, P], F32, name="norm_rows")
         identity = keep.tile([P, P], F32, name="identity")
@@ -58,22 +58,23 @@ def tile_attend_pq_lin_bias_kernel(tc, qT, cb, norm, bias, offs, out):
         nc.scalar.copy(norm_sb[:], norm_spread[:].rearrange("p u n -> p (u n)"))
 
         grouped = keep.tile([P, 4 * P, PACK], BF16, name="grouped", align_bytes=64)
-        codes = keep.tile([P, 4 * P], U32, name="codes", align_bytes=64)
         scales = keep.tile([P, 4 * P], U8, name="scales", align_bytes=64)
+        q_start = (0, 3 * P)
+        k_start = (P, 2 * P)
         gathered = [keep.tile([P, HALF], F32, name=f"gathered{h}") for h in range(2)]
         acc = [[psum.tile([P, HALF], F32, name=f"acc{h}{b}") for b in range(2)] for h in range(2)]
         result = [[keep.tile([P, HALF], F32, name=f"result{h}{b}") for b in range(2)] for h in range(2)]
 
-        def quantize(first, last):
+        def quantize(codes, first, last):
             nc.vector.quantize_mx(
-                out=codes[:, first:last].bitcast(FP8X4),
+                out=codes[:].bitcast(FP8X4),
                 scales=scales[:, first:last],
                 in_=grouped[:, first:last, :].rearrange("p n t -> p (n t)"),
             )
 
         def interleave(copy, b, first, last):
             copy(
-                grouped[:, N + P * b + first : N + P * b + last, :].rearrange("p (c i) t -> p c t i", i=4),
+                grouped[:, q_start[b] + first : q_start[b] + last, :].rearrange("p (c i) t -> p c t i", i=4),
                 q_raw[b][:, :, first:last].rearrange("p t (c i) -> p c t i", i=4),
             )
 
@@ -86,23 +87,26 @@ def tile_attend_pq_lin_bias_kernel(tc, qT, cb, norm, bias, offs, out):
                     MULT,
                 )
             for h in range(2):
-                nc.vector.tensor_copy(grouped[:, HALF * h : HALF * h + HALF, t], gathered[h][:])
+                nc.vector.tensor_copy(grouped[:, k_start[h] : k_start[h] + HALF, t], gathered[h][:])
         interleave(nc.scalar.copy, 0, 0, P)
         interleave(nc.scalar.copy, 1, 0, SCALAR_SHARE)
-        quantize(0, P)
         interleave(nc.vector.tensor_copy, 1, SCALAR_SHARE, P)
-        quantize(P, 3 * P)
-        quantize(3 * P, 4 * P)
+        first_codes = keep.tile([P, 2 * P], U32, name="first_codes", align_bytes=64)
+        k1_codes = keep.tile([P, P], U32, name="k1_codes", tag="q_raw0", align_bytes=64)
+        q1_codes = keep.tile([P, P], U32, name="q1_codes", align_bytes=64)
+        quantize(first_codes, 0, 2 * P)
+        quantize(k1_codes, 2 * P, 3 * P)
+        quantize(q1_codes, 3 * P, 4 * P)
+        q_codes = (first_codes[:, 0:P], q1_codes[:])
+        k_codes = (first_codes[:, P : 2 * P], k1_codes[:])
         for b in range(2):
-            q_cols = slice(N + P * b, N + P * b + P)
             for h in range(2):
-                n_cols = slice(HALF * h, HALF * h + HALF)
                 nc.tensor.matmul_mx(
                     out=acc[h][b][:],
-                    lhsT=codes[:, q_cols].bitcast(FP8X4),
-                    lhsT_scale=scales[:, q_cols],
-                    rhs=codes[:, n_cols].bitcast(FP8X4),
-                    rhs_scale=scales[:, n_cols],
+                    lhsT=q_codes[b].bitcast(FP8X4),
+                    lhsT_scale=scales[:, q_start[b] : q_start[b] + P],
+                    rhs=k_codes[h].bitcast(FP8X4),
+                    rhs_scale=scales[:, k_start[h] : k_start[h] + HALF],
                     start=True,
                     stop=True,
                 )

@@ -28,8 +28,9 @@ def tile_attend_pq_lin_bias_kernel(tc, qT, cb, norm, bias, offs, out):
     ):
         planes = [keep.tile([P, 4096], F32, name=f"plane{t}") for t in range(PACK)]
         lists = keep.tile([P, N // 16], U16, name="lists")
-        norm_sb = keep.tile([P, N], F32, name="norm_sb")
-        bias_sb = keep.tile([P, N], F32, name="bias_sb")
+        spread = keep.tile([P, 2 * N], F32, name="spread")
+        norm_sb = spread[:, 0:N]
+        bias_sb = spread[:, N : 2 * N]
         q_raw = [keep.tile([P, PACK, P], F32, name=f"q_raw{b}", tag=f"q_raw{b}", align_bytes=64) for b in range(2)]
 
         norm_rows = keep.tile([P, P], F32, name="norm_rows")
@@ -41,21 +42,21 @@ def tile_attend_pq_lin_bias_kernel(tc, qT, cb, norm, bias, offs, out):
         nc.sync.dma_start(planes[0][:], cb_rows[:, 0, :])
         nc.sync.dma_start(lists[:], offs)
         nc.sync.dma_start(norm_rows[0:2, :], norm[0:1, :].rearrange("o (u n) -> (o u) n", u=2))
+        nc.sync.dma_start(norm_rows[2:4, :], bias[0:1, :].rearrange("o (u n) -> (o u) n", u=2))
         for t in range(1, PACK):
             nc.sync.dma_start(planes[t][:], cb_rows[:, t, :])
         q_rows = qT[0, :, :].rearrange("(p t) q -> p t q", t=PACK)
         for b in range(2):
             nc.sync.dma_start(q_raw[b][:], q_rows[:, :, P * b : P * b + P])
-        nc.sync.dma_start(bias_sb[:], bias)
 
         norm_turned = psum.tile([P, P], F32, name="norm_turned")
-        norm_cols = keep.tile([P, 2], F32, name="norm_cols")
-        norm_spread = psum.tile([P, 2, P], F32, name="norm_spread")
+        norm_cols = keep.tile([P, 4], F32, name="norm_cols")
+        norm_spread = psum.tile([P, 4, P], F32, name="norm_spread")
         nc.tensor.transpose(norm_turned[:], norm_rows[:], identity[:])
-        nc.scalar.copy(norm_cols[:], norm_turned[:, 0:2])
-        for u in range(2):
+        nc.scalar.copy(norm_cols[:], norm_turned[:, 0:4])
+        for u in range(4):
             nc.tensor.transpose(norm_spread[:, u, :], norm_cols[:, u : u + 1].to_broadcast([P, P]), identity[:])
-        nc.scalar.copy(norm_sb[:], norm_spread[:].rearrange("p u n -> p (u n)"))
+        nc.scalar.copy(spread[:], norm_spread[:].rearrange("p u n -> p (u n)"))
 
         grouped = keep.tile([P, 4 * P, PACK], BF16, name="grouped", align_bytes=64)
         scales = keep.tile([P, 4 * P], U8, name="scales", align_bytes=64)

@@ -1,5 +1,4 @@
 import concourse.mybir as mybir
-from concourse.masks import make_identity
 
 F32 = mybir.dt.float32
 BF16 = mybir.dt.bfloat16
@@ -28,35 +27,33 @@ def tile_attend_pq_lin_bias_kernel(tc, qT, cb, norm, bias, offs, out):
     ):
         planes = [keep.tile([P, 4096], F32, name=f"plane{t}") for t in range(PACK)]
         lists = keep.tile([P, N // 16], U16, name="lists")
-        spread = keep.tile([P, 2 * N], F32, name="spread")
+        spread = keep.tile([P, 2 * N], F32, name="spread", align_bytes=64)
         norm_sb = spread[:, 0:N]
         bias_sb = spread[:, N : 2 * N]
         q_raw = [keep.tile([P, PACK, P], F32, name=f"q_raw{b}", tag=f"q_raw{b}", align_bytes=64) for b in range(2)]
 
-        norm_rows = keep.tile([P, P], F32, name="norm_rows")
-        identity = keep.tile([P, P], F32, name="identity")
-        nc.gpsimd.memset(norm_rows[:], 0.0)
-        make_identity(nc, identity[:])
+        rows = keep.tile([P, 2 * N], F32, name="rows", align_bytes=64)
+        nc.gpsimd.memset(rows[:], 0.0)
 
         cb_rows = cb.rearrange("(p t) c -> p t c", t=PACK)
         nc.sync.dma_start(planes[0][:], cb_rows[:, 0, :])
         nc.sync.dma_start(lists[:], offs)
-        nc.sync.dma_start(norm_rows[0:2, :], norm[0:1, :].rearrange("o (u n) -> (o u) n", u=2))
-        nc.sync.dma_start(norm_rows[2:4, :], bias[0:1, :].rearrange("o (u n) -> (o u) n", u=2))
+        nc.sync.dma_start(rows[0:P:32, 0:N], norm[0:4, :])
+        nc.sync.dma_start(rows[0:P:32, N : 2 * N], bias[0:4, :])
         for t in range(1, PACK):
             nc.sync.dma_start(planes[t][:], cb_rows[:, t, :])
         q_rows = qT[0, :, :].rearrange("(p t) q -> p t q", t=PACK)
         for b in range(2):
             nc.sync.dma_start(q_raw[b][:], q_rows[:, :, P * b : P * b + P])
 
-        norm_turned = psum.tile([P, P], F32, name="norm_turned")
-        norm_cols = keep.tile([P, 4], F32, name="norm_cols")
-        norm_spread = psum.tile([P, 4, P], F32, name="norm_spread")
-        nc.tensor.transpose(norm_turned[:], norm_rows[:], identity[:])
-        nc.scalar.copy(norm_cols[:], norm_turned[:, 0:4])
-        for u in range(4):
-            nc.tensor.transpose(norm_spread[:, u, :], norm_cols[:, u : u + 1].to_broadcast([P, P]), identity[:])
-        nc.scalar.copy(spread[:], norm_spread[:].rearrange("p u n -> p (u n)"))
+        turned = keep.tile([P, 2 * N], F32, name="turned", align_bytes=64)
+        repeated = keep.tile([P, 2 * N], F32, name="repeated", align_bytes=64)
+        nc.vector.transpose(turned[:], rows[:])
+        nc.vector.tensor_copy(
+            repeated[:].rearrange("p (j e) -> p j e", e=32),
+            turned[:].rearrange("p (j e) -> p j e", e=32)[:, :, 0:1].to_broadcast([P, 2 * N // 32, 32]),
+        )
+        nc.vector.transpose(spread[:], repeated[:])
 
         grouped = keep.tile([P, 4 * P, PACK], BF16, name="grouped", align_bytes=64)
         scales = keep.tile([P, 4 * P], U8, name="scales", align_bytes=64)

@@ -65,7 +65,7 @@ def tile_attend_pq_lin_bias_kernel(tc, qT, cb, norm, bias, offs, out):
 
         def quantize(codes, first, last):
             nc.vector.quantize_mx(
-                out=codes[:].bitcast(FP8X4),
+                out=codes.bitcast(FP8X4),
                 scales=scales[:, first:last],
                 in_=grouped[:, first:last, :].rearrange("p n t -> p (n t)"),
             )
@@ -92,9 +92,10 @@ def tile_attend_pq_lin_bias_kernel(tc, qT, cb, norm, bias, offs, out):
         first_codes = keep.tile([P, 2 * P], U32, name="first_codes", align_bytes=64)
         k1_codes = keep.tile([P, P], U32, name="k1_codes", tag="q_raw0", align_bytes=64)
         q1_codes = keep.tile([P, P], U32, name="q1_codes", align_bytes=64)
-        quantize(first_codes, 0, 2 * P)
-        quantize(k1_codes, 2 * P, 3 * P)
-        quantize(q1_codes, 3 * P, 4 * P)
+        quantize(first_codes[:, P : 2 * P], P, 2 * P)
+        quantize(first_codes[:, 0:P], 0, P)
+        quantize(k1_codes[:], 2 * P, 3 * P)
+        quantize(q1_codes[:], 3 * P, 4 * P)
         q_codes = (first_codes[:, 0:P], q1_codes[:])
         k_codes = (first_codes[:, P : 2 * P], k1_codes[:])
         for b in range(2):

@@ -59,7 +59,7 @@ def tile_attend_pq_lin_bias_kernel(tc, qT, cb, norm, bias, offs, out):
         scales = keep.tile([P, 4 * P], U8, name="scales", align_bytes=64)
         q_start = (0, 3 * P)
         k_start = (P, 2 * P)
-        gathered = [keep.tile([P, HALF], F32, name=f"gathered{h}") for h in range(2)]
+        gathered = [[keep.tile([P, HALF], F32, name=f"gathered{t}{h}") for h in range(2)] for t in range(PACK)]
         acc = [[psum.tile([P, HALF], F32, name=f"acc{h}{b}") for b in range(2)] for h in range(2)]
         result = [[keep.tile([P, HALF], F32, name=f"result{h}{b}") for b in range(2)] for h in range(2)]
 
@@ -79,13 +79,13 @@ def tile_attend_pq_lin_bias_kernel(tc, qT, cb, norm, bias, offs, out):
         for t in range(PACK):
             for h in range(2):
                 nc.vector.tensor_tensor(
-                    gathered[h][:],
+                    gathered[t][h][:],
                     planes[t][:].indirect(lists[:, 8 * h : 8 * h + 8]),
                     norm_sb[:, HALF * h : HALF * h + HALF],
                     MULT,
                 )
             for h in range(2):
-                nc.vector.tensor_copy(grouped[:, k_start[h] : k_start[h] + HALF, t], gathered[h][:])
+                nc.vector.tensor_copy(grouped[:, k_start[h] : k_start[h] + HALF, t], gathered[t][h][:])
         interleave(nc.scalar.copy, 0, 0, P)
         interleave(nc.scalar.copy, 1, 0, SCALAR_SHARE)
         interleave(nc.vector.tensor_copy, 1, SCALAR_SHARE, P)

@@ -36,15 +36,19 @@ def tile_attend_pq_lin_bias_kernel(tc, qT, cb, norm, bias, offs, out):
         nc.gpsimd.memset(rows[:], 0.0)
 
         cb_rows = cb.rearrange("(p t) c -> p t c", t=PACK)
-        nc.sync.dma_start(planes[0][:], cb_rows[:, 0, :])
+        pair = keep.tile([P, 2, 4096], F32, name="pair")
+        nc.sync.dma_start(pair[:], cb_rows[:, 0:2, :])
         nc.sync.dma_start(lists[:], offs)
         nc.sync.dma_start(rows[0:P:32, 0:N], norm[0:4, :])
         nc.sync.dma_start(rows[0:P:32, N : 2 * N], bias[0:4, :])
-        for t in range(1, PACK):
+        for t in range(2, PACK):
             nc.sync.dma_start(planes[t][:], cb_rows[:, t, :])
         q_rows = qT[0, :, :].rearrange("(p t) q -> p t q", t=PACK)
         for b in range(2):
             nc.sync.dma_start(q_raw[b][:], q_rows[:, :, P * b : P * b + P])
+
+        nc.vector.tensor_copy(planes[0][:], pair[:, 0, :])
+        nc.scalar.copy(planes[1][:], pair[:, 1, :])
 
         turned = keep.tile([P, 2 * N], F32, name="turned", align_bytes=64)
         repeated = keep.tile([P, 2 * N], F32, name="repeated", align_bytes=64)

@@ -39,8 +39,10 @@ def tile_attend_pq_lin_bias_kernel(tc, qT, cb, norm, bias, offs, out):
         pair = keep.tile([P, 2, 4096], F32, name="pair")
         nc.sync.dma_start(pair[:], cb_rows[:, 0:2, :])
         nc.sync.dma_start(lists[:], offs)
-        nc.sync.dma_start(rows[0:P:32, 0:N], norm[0:4, :])
-        nc.sync.dma_start(rows[0:P:32, N : 2 * N], bias[0:4, :])
+        for first, last in ((0, 64), (64, 128), (128, 256)):
+            nc.sync.dma_start(rows[0:P:32, first:last], norm[0:4, first:last])
+        for h in range(2):
+            nc.sync.dma_start(rows[0:P:32, N + HALF * h : N + HALF * h + HALF], bias[0:4, HALF * h : HALF * h + HALF])
         for t in range(2, PACK):
             nc.sync.dma_start(planes[t][:], cb_rows[:, t, :])
         q_rows = qT[0, :, :].rearrange("(p t) q -> p t q", t=PACK)

@@ -25,18 +25,18 @@ def tile_attend_pq_lin_bias_kernel(tc, qT, cb, norm, bias, offs, out):
         tc.tile_pool(name="keep", bufs=1) as keep,
         tc.psum_pool(name="psum", bufs=1) as psum,
     ):
-        planes = [keep.tile([P, 4096], F32, name=f"plane{t}") for t in range(PACK)]
+        planes = [keep.tile([P, 4096], F32, name=f"plane{t}", align_bytes=256) for t in range(PACK)]
         lists = keep.tile([P, N // 16], U16, name="lists")
-        spread = keep.tile([P, 2 * N], F32, name="spread", align_bytes=64)
+        spread = keep.tile([P, 2 * N], F32, name="spread", align_bytes=256)
         norm_sb = spread[:, 0:N]
         bias_sb = spread[:, N : 2 * N]
-        q_raw = [keep.tile([P, PACK, P], F32, name=f"q_raw{b}", tag=f"q_raw{b}", align_bytes=64) for b in range(2)]
+        q_raw = [keep.tile([P, PACK, P], F32, name=f"q_raw{b}", tag=f"q_raw{b}", align_bytes=256) for b in range(2)]
 
-        rows = keep.tile([P, 2 * N], F32, name="rows", align_bytes=64)
+        rows = keep.tile([P, 2 * N], F32, name="rows", align_bytes=256)
         nc.gpsimd.memset(rows[:], 0.0)
 
         cb_rows = cb.rearrange("(p t) c -> p t c", t=PACK)
-        pair = keep.tile([P, 2, 4096], F32, name="pair")
+        pair = keep.tile([P, 2, 4096], F32, name="pair", align_bytes=256)
         nc.sync.dma_start(pair[:], cb_rows[:, 0:2, :])
         nc.sync.dma_start(lists[:], offs)
         for first, last in ((0, 64), (64, 128), (128, 256)):
@@ -52,8 +52,8 @@ def tile_attend_pq_lin_bias_kernel(tc, qT, cb, norm, bias, offs, out):
         nc.vector.tensor_copy(planes[0][:], pair[:, 0, :])
         nc.scalar.copy(planes[1][:], pair[:, 1, :])
 
-        turned = keep.tile([P, 2 * N], F32, name="turned", align_bytes=64)
-        repeated = keep.tile([P, 2 * N], F32, name="repeated", align_bytes=64)
+        turned = keep.tile([P, 2 * N], F32, name="turned", align_bytes=256)
+        repeated = keep.tile([P, 2 * N], F32, name="repeated", align_bytes=256)
         nc.vector.transpose(turned[:], rows[:])
         nc.vector.tensor_copy(
             repeated[:].rearrange("p (j e) -> p j e", e=32),
@@ -61,13 +61,13 @@ def tile_attend_pq_lin_bias_kernel(tc, qT, cb, norm, bias, offs, out):
         )
         nc.vector.transpose(spread[:], repeated[:])
 
-        grouped = keep.tile([P, 4 * P, PACK], BF16, name="grouped", align_bytes=64)
-        scales = keep.tile([P, 4 * P], U8, name="scales", align_bytes=64)
+        grouped = keep.tile([P, 4 * P, PACK], BF16, name="grouped", align_bytes=256)
+        scales = keep.tile([P, 4 * P], U8, name="scales", align_bytes=256)
         q_start = (0, 3 * P)
         k_start = (P, 2 * P)
-        gathered = [[keep.tile([P, HALF], F32, name=f"gathered{t}{h}") for h in range(2)] for t in range(PACK)]
+        gathered = [[keep.tile([P, HALF], F32, name=f"gathered{t}{h}", align_bytes=256) for h in range(2)] for t in range(PACK)]
         acc = [[psum.tile([P, HALF], F32, name=f"acc{h}{b}") for b in range(2)] for h in range(2)]
-        result = [[keep.tile([P, HALF], F32, name=f"result{h}{b}") for b in range(2)] for h in range(2)]
+        result = [[keep.tile([P, HALF], F32, name=f"result{h}{b}", align_bytes=256) for b in range(2)] for h in range(2)]
 
         def quantize(codes, first, last):
             nc.vector.quantize_mx(
@@ -95,9 +95,9 @@ def tile_attend_pq_lin_bias_kernel(tc, qT, cb, norm, bias, offs, out):
         interleave(nc.scalar.copy, 0, 0, P)
         interleave(nc.scalar.copy, 1, 0, SCALAR_SHARE)
         interleave(nc.vector.tensor_copy, 1, SCALAR_SHARE, P)
-        first_codes = keep.tile([P, 2 * P], U32, name="first_codes", align_bytes=64)
-        k1_codes = keep.tile([P, P], U32, name="k1_codes", tag="q_raw0", align_bytes=64)
-        q1_codes = keep.tile([P, P], U32, name="q1_codes", align_bytes=64)
+        first_codes = keep.tile([P, 2 * P], U32, name="first_codes", align_bytes=256)
+        k1_codes = keep.tile([P, P], U32, name="k1_codes", tag="q_raw0", align_bytes=256)
+        q1_codes = keep.tile([P, P], U32, name="q1_codes", align_bytes=256)
         quantize(first_codes[:, P : 2 * P], P, 2 * P)
         quantize(first_codes[:, 0:P], 0, P)
         quantize(k1_codes[:], 2 * P, 3 * P)

@@ -25,18 +25,18 @@ def tile_attend_pq_lin_bias_kernel(tc, qT, cb, norm, bias, offs, out):
         tc.tile_pool(name="keep", bufs=1) as keep,
         tc.psum_pool(name="psum", bufs=1) as psum,
     ):
-        planes = [keep.tile([P, 4096], F32, name=f"plane{t}", align_bytes=256) for t in range(PACK)]
+        planes = [keep.tile([P, 4096], F32, name=f"plane{t}", align_bytes=4096) for t in range(PACK)]
         lists = keep.tile([P, N // 16], U16, name="lists")
         spread = keep.tile([P, 2 * N], F32, name="spread", align_bytes=256)
         norm_sb = spread[:, 0:N]
         bias_sb = spread[:, N : 2 * N]
-        q_raw = [keep.tile([P, PACK, P], F32, name=f"q_raw{b}", tag=f"q_raw{b}", align_bytes=256) for b in range(2)]
+        q_raw = [keep.tile([P, PACK, P], F32, name=f"q_raw{b}", tag=f"q_raw{b}", align_bytes=2048) for b in range(2)]
 
         rows = keep.tile([P, 2 * N], F32, name="rows", align_bytes=256)
         nc.gpsimd.memset(rows[:], 0.0)
 
         cb_rows = cb.rearrange("(p t) c -> p t c", t=PACK)
-        pair = keep.tile([P, 2, 4096], F32, name="pair", align_bytes=256)
+        pair = keep.tile([P, 2, 4096], F32, name="pair", align_bytes=4096)
         nc.sync.dma_start(pair[:], cb_rows[:, 0:2, :])
         nc.sync.dma_start(lists[:], offs)
         for first, last in ((0, 64), (64, 128), (128, 256)):
@@ -67,7 +67,7 @@ def tile_attend_pq_lin_bias_kernel(tc, qT, cb, norm, bias, offs, out):
         k_start = (P, 2 * P)
         gathered = [[keep.tile([P, HALF], F32, name=f"gathered{t}{h}", align_bytes=256) for h in range(2)] for t in range(PACK)]
         acc = [[psum.tile([P, HALF], F32, name=f"acc{h}{b}") for b in range(2)] for h in range(2)]
-        result = [[keep.tile([P, HALF], F32, name=f"result{h}{b}", align_bytes=256) for b in range(2)] for h in range(2)]
+        result = [[keep.tile([P, HALF], F32, name=f"result{h}{b}", align_bytes=512) for b in range(2)] for h in range(2)]
 
         def quantize(codes, first, last):
             nc.vector.quantize_mx(
@@ -96,7 +96,7 @@ def tile_attend_pq_lin_bias_kernel(tc, qT, cb, norm, bias, offs, out):
         interleave(nc.scalar.copy, 1, 0, SCALAR_SHARE)
         interleave(nc.vector.tensor_copy, 1, SCALAR_SHARE, P)
         first_codes = keep.tile([P, 2 * P], U32, name="first_codes", align_bytes=256)
-        k1_codes = keep.tile([P, P], U32, name="k1_codes", tag="q_raw0", align_bytes=256)
+        k1_codes = keep.tile([P, P], U32, name="k1_codes", tag="q_raw0", align_bytes=2048)
         q1_codes = keep.tile([P, P], U32, name="q1_codes", align_bytes=256)
         quantize(first_codes[:, P : 2 * P], P, 2 * P)
         quantize(first_codes[:, 0:P], 0, P)

@@ -15,7 +15,7 @@ N = 256
 NQ = 256
 D = 512
 HALF = 128
-SCALAR_SHARE = 64
+SCALAR_SHARE = 96
 FLOPS = 2 * NQ * N * D
 
 
@@ -67,7 +67,6 @@ def tile_attend_pq_lin_bias_kernel(tc, qT, cb, norm, bias, offs, out):
         k_start = (P, 2 * P)
         gathered = [[keep.tile([P, HALF], F32, name=f"gathered{t}{h}", align_bytes=256) for h in range(2)] for t in range(PACK)]
         acc = [[psum.tile([P, HALF], F32, name=f"acc{h}{b}") for b in range(2)] for h in range(2)]
-        result = [[keep.tile([P, HALF], F32, name=f"result{h}{b}", align_bytes=512) for b in range(2)] for h in range(2)]
 
         def quantize(codes, first, last):
             nc.vector.quantize_mx(
@@ -115,9 +114,13 @@ def tile_attend_pq_lin_bias_kernel(tc, qT, cb, norm, bias, offs, out):
                     start=True,
                     stop=True,
                 )
+        result = [
+            keep.tile([P, N], F32, name="result0", tag="q_raw1", align_bytes=2048),
+            keep.tile([P, N], F32, name="result1", align_bytes=512),
+        ]
         for b in range(2):
             for h in range(2):
                 n_cols = slice(HALF * h, HALF * h + HALF)
-                nc.vector.tensor_tensor(result[h][b][:], acc[h][b][:], bias_sb[:, n_cols], ADD)
+                nc.vector.tensor_tensor(result[b][:, n_cols], acc[h][b][:], bias_sb[:, n_cols], ADD)
                 store = nc.scalar if h == 0 else nc.sync
-                store.dma_start(out[0, P * b : P * b + P, n_cols], result[h][b][:])
+                store.dma_start(out[0, P * b : P * b + P, n_cols], result[b][:, n_cols])

@@ -92,7 +92,8 @@ def tile_attend_pq_lin_bias_kernel(tc, qT, cb, norm, bias, offs, out):
             for h in range(2):
                 nc.vector.tensor_copy(grouped[:, k_start[h] : k_start[h] + HALF, t], gathered[t][h][:])
         interleave(nc.scalar.copy, 0, 0, P)
-        interleave(nc.scalar.copy, 1, 0, SCALAR_SHARE)
+        interleave(nc.scalar.copy, 1, 0, 64)
+        interleave(nc.scalar.copy, 1, 64, SCALAR_SHARE)
         interleave(nc.vector.tensor_copy, 1, SCALAR_SHARE, P)
         first_codes = keep.tile([P, 2 * P], U32, name="first_codes", align_bytes=256)
         k1_codes = keep.tile([P, P], U32, name="k1_codes", tag="q_raw0", align_bytes=2048)
@@ -100,7 +101,8 @@ def tile_attend_pq_lin_bias_kernel(tc, qT, cb, norm, bias, offs, out):
         quantize(first_codes[:, P : 2 * P], P, 2 * P)
         quantize(first_codes[:, 0:P], 0, P)
         quantize(k1_codes[:], 2 * P, 3 * P)
-        quantize(q1_codes[:], 3 * P, 4 * P)
+        quantize(q1_codes[:, 0:64], 3 * P, 3 * P + 64)
+        quantize(q1_codes[:, 64:P], 3 * P + 64, 4 * P)
         q_codes = (first_codes[:, 0:P], q1_codes[:])
         k_codes = (first_codes[:, P : 2 * P], k1_codes[:])
         for b in range(2):

import concourse.mybir as mybir

F32 = mybir.dt.float32
BF16 = mybir.dt.bfloat16
U32 = mybir.dt.uint32
U16 = mybir.dt.uint16
U8 = mybir.dt.uint8
FP8X4 = mybir.dt.float8_e4m3fn_x4
MULT = mybir.AluOpType.mult
ADD = mybir.AluOpType.add

P = 128
PACK = 4
N = 256
NQ = 256
D = 512
HALF = 128
SCALAR_SHARE = 96
FLOPS = 2 * NQ * N * D


def tile_attend_pq_lin_bias_kernel(tc, qT, cb, norm, bias, offs, out):
    nc = tc.nc
    with (
        tc.tile_pool(name="keep", bufs=1) as keep,
        tc.psum_pool(name="psum", bufs=1) as psum,
    ):
        planes = [keep.tile([P, 4096], F32, name=f"plane{t}", align_bytes=4096) for t in range(PACK)]
        lists = keep.tile([P, N // 16], U16, name="lists")
        spread = keep.tile([P, 2 * N], F32, name="spread", align_bytes=256)
        norm_sb = spread[:, 0:N]
        bias_sb = spread[:, N : 2 * N]
        q_raw = [keep.tile([P, PACK, P], F32, name=f"q_raw{b}", tag=f"q_raw{b}", align_bytes=2048) for b in range(2)]

        rows = keep.tile([P, 2 * N], F32, name="rows", align_bytes=256)
        nc.gpsimd.memset(rows[:], 0.0)

        cb_rows = cb.rearrange("(p t) c -> p t c", t=PACK)
        pair = keep.tile([P, 2, 4096], F32, name="pair", align_bytes=4096)
        nc.sync.dma_start(pair[:], cb_rows[:, 0:2, :])
        nc.sync.dma_start(lists[:], offs)
        for first, last in ((0, 64), (64, 128), (128, 256)):
            nc.sync.dma_start(rows[0:P:32, first:last], norm[0:4, first:last])
        for h in range(2):
            nc.sync.dma_start(rows[0:P:32, N + HALF * h : N + HALF * h + HALF], bias[0:4, HALF * h : HALF * h + HALF])
        for t in range(2, PACK):
            nc.sync.dma_start(planes[t][:], cb_rows[:, t, :])
        q_rows = qT[0, :, :].rearrange("(p t) q -> p t q", t=PACK)
        for b in range(2):
            nc.sync.dma_start(q_raw[b][:], q_rows[:, :, P * b : P * b + P])

        nc.vector.tensor_copy(planes[0][:], pair[:, 0, :])
        nc.scalar.copy(planes[1][:], pair[:, 1, :])

        turned = keep.tile([P, 2 * N], F32, name="turned", align_bytes=256)
        repeated = keep.tile([P, 2 * N], F32, name="repeated", align_bytes=256)
        nc.vector.transpose(turned[:], rows[:])
        nc.vector.tensor_copy(
            repeated[:].rearrange("p (j e) -> p j e", e=32),
            turned[:].rearrange("p (j e) -> p j e", e=32)[:, :, 0:1].to_broadcast([P, 2 * N // 32, 32]),
        )
        nc.vector.transpose(spread[:], repeated[:])

        grouped = keep.tile([P, 4 * P, PACK], BF16, name="grouped", align_bytes=256)
        scales = keep.tile([P, 4 * P], U8, name="scales", align_bytes=256)
        q_start = (0, 3 * P)
        k_start = (P, 2 * P)
        gathered = [[keep.tile([P, HALF], F32, name=f"gathered{t}{h}", align_bytes=256) for h in range(2)] for t in range(PACK)]
        acc = [[psum.tile([P, HALF], F32, name=f"acc{h}{b}") for b in range(2)] for h in range(2)]

        def quantize(codes, first, last):
            nc.vector.quantize_mx(
                out=codes.bitcast(FP8X4),
                scales=scales[:, first:last],
                in_=grouped[:, first:last, :].rearrange("p n t -> p (n t)"),
            )

        def interleave(copy, b, first, last):
            copy(
                grouped[:, q_start[b] + first : q_start[b] + last, :].rearrange("p (c i) t -> p c t i", i=4),
                q_raw[b][:, :, first:last].rearrange("p t (c i) -> p c t i", i=4),
            )

        for t in range(PACK):
            for h in range(2):
                nc.vector.tensor_tensor(
                    gathered[t][h][:],
                    planes[t][:].indirect(lists[:, 8 * h : 8 * h + 8]),
                    norm_sb[:, HALF * h : HALF * h + HALF],
                    MULT,
                )
            for h in range(2):
                nc.vector.tensor_copy(grouped[:, k_start[h] : k_start[h] + HALF, t], gathered[t][h][:])
        interleave(nc.scalar.copy, 0, 0, P)
        interleave(nc.scalar.copy, 1, 0, 64)
        interleave(nc.scalar.copy, 1, 64, SCALAR_SHARE)
        interleave(nc.vector.tensor_copy, 1, SCALAR_SHARE, P)
        first_codes = keep.tile([P, 2 * P], U32, name="first_codes", align_bytes=256)
        k1_codes = keep.tile([P, P], U32, name="k1_codes", tag="q_raw0", align_bytes=2048)
        q1_codes = keep.tile([P, P], U32, name="q1_codes", align_bytes=256)
        quantize(first_codes[:, P : 2 * P], P, 2 * P)
        quantize(first_codes[:, 0:P], 0, P)
        quantize(k1_codes[:], 2 * P, 3 * P)
        quantize(q1_codes[:, 0:64], 3 * P, 3 * P + 64)
        quantize(q1_codes[:, 64:P], 3 * P + 64, 4 * P)
        q_codes = (first_codes[:, 0:P], q1_codes[:])
        k_codes = (first_codes[:, P : 2 * P], k1_codes[:])
        for b in range(2):
            for h in range(2):
                nc.tensor.matmul_mx(
                    out=acc[h][b][:],
                    lhsT=q_codes[b].bitcast(FP8X4),
                    lhsT_scale=scales[:, q_start[b] : q_start[b] + P],
                    rhs=k_codes[h].bitcast(FP8X4),
                    rhs_scale=scales[:, k_start[h] : k_start[h] + HALF],
                    start=True,
                    stop=True,
                )
        result = [
            keep.tile([P, N], F32, name="result0", tag="q_raw1", align_bytes=2048),
            keep.tile([P, N], F32, name="result1", align_bytes=512),
        ]
        for b in range(2):
            for h in range(2):
                n_cols = slice(HALF * h, HALF * h + HALF)
                nc.vector.tensor_tensor(result[b][:, n_cols], acc[h][b][:], bias_sb[:, n_cols], ADD)
                store = nc.scalar if h == 0 else nc.sync
                store.dma_start(out[0, P * b : P * b + P, n_cols], result[b][:, n_cols])
